import numpy as np
import ml_dtypes


def mxq(x, axis, fmt="e4m3"):
    dtype, down = {"e4m3": (ml_dtypes.float8_e4m3fn, 7), "e5m2": (ml_dtypes.float8_e5m2, 14)}[fmt]
    v = np.moveaxis(np.asarray(x, np.float32).astype(ml_dtypes.bfloat16).astype(np.float64), axis, -1)
    blocks = v.reshape(v.shape[:-1] + (-1, 32))
    amax = np.abs(blocks).max(-1, keepdims=True)
    byte = np.maximum(np.where(amax > 0, np.frexp(amax)[1] - 1 + 127, 0) - down, 1)
    scale = np.exp2(byte - 127.0)
    codes = (blocks / scale).astype(np.float32).astype(dtype).astype(np.float64)
    return np.moveaxis((codes * scale).reshape(v.shape), -1, axis)


WIDE = False


def mx_kscale(k):
    if not WIDE:
        return np.ones(k)
    levels = np.array([10, -10, 5, -5, 0])
    if k % 512:
        return np.exp2(np.random.permutation(np.resize(levels, k // 32))).repeat(32)
    a = np.empty((k // 512, 16))
    for p in range(k // 512):
        a[p, :8] = np.random.permutation(np.resize(levels, 8))
        for g in range(8):
            far = levels[np.abs(levels - a[p, g]) >= 10]
            a[p, g + 8] = far[np.random.randint(len(far))]
    return np.exp2(a.ravel()).repeat(32)


def f64(x):
    return np.asarray(x).astype(np.float64)


def striped(idx):
    return np.tile(idx.reshape(-1, 16).T, (8, 1)).astype(np.uint16)


def unstriped(offs):
    return offs[:16].T.reshape(-1).astype(np.int64)


E2M1 = np.array([0.0, 0.5, 1.0, 1.5, 2.0, 3.0, 4.0, 6.0, -0.0, -0.5, -1.0, -1.5, -2.0, -3.0, -4.0, -6.0])


def pack_fp4(w):
    k, n = w.shape
    w = f64(np.asarray(w, np.float32).astype(ml_dtypes.bfloat16)).reshape(k // 32, 32, n)
    amax = np.abs(w).max(1)
    mant, ex = np.frexp(amax / 6.0)
    byte = np.clip(np.where(amax > 0, np.where(mant > 0.5, ex, ex - 1) + 127, 1), 1, 254)
    scaled = (w * np.exp2(127.0 - byte)[:, None, :]).reshape(k, n).astype(np.float32)
    c = np.ascontiguousarray(scaled.reshape(k // 512, 128, 4, n).transpose(0, 1, 3, 2)).astype(ml_dtypes.float4_e2m1fn).view(np.uint8) & 0xF
    words = (c[..., 0::2] | (c[..., 1::2] << 4)).reshape(k // 512, 128, 2 * n)
    return np.ascontiguousarray(words), np.ascontiguousarray(byte.astype(np.uint8).reshape(k // 512, 16, n))


def unpack_fp4(words, scales):
    g, _, n = scales.shape
    words = np.ascontiguousarray(words).reshape(g, 128, n, 2)
    nib = np.empty((g, 128, n, 4), np.uint8)
    nib[..., 0::2] = words & 0xF
    nib[..., 1::2] = words >> 4
    vals = E2M1[nib] * np.repeat(np.exp2(scales.astype(np.float64) - 127.0), 8, axis=1)[..., None]
    return vals.transpose(0, 1, 3, 2).reshape(g * 512, n)


K, T, S, V, N = 1024, 2048, 1024, 512, 128


def setup_inputs():
    n = np.random.standard_normal
    s = mx_kscale(K)[:, None]
    packed_w1 = pack_fp4(n((K, N)) / np.sqrt(K) / s)
    return {
        "xT": (n((K, T)) * s).astype(np.float32),
        "w1_words": packed_w1[0],
        "w1_scales": packed_w1[1],
        "offs": striped(np.random.permutation(T)[:S]),
    }


def reference(xT, w1_words, w1_scales, offs):
    xq = mxq(f64(xT)[:, unstriped(offs)], 0, "e4m3")
    e = np.exp(unpack_fp4(w1_words, w1_scales).T @ xq)
    return np.log(e[:, :V] + e[:, V:2 * V])

@@ -1,0 +1,170 @@
+from contextlib import ExitStack
+
+import concourse.mybir as mybir
+
+K, T, S, V, N = 1024, 2048, 1024, 512, 128
+FLOPS = 2 * K * S * N
+
+F32 = mybir.dt.float32
+BF16 = mybir.dt.bfloat16
+U32 = mybir.dt.uint32
+I32 = mybir.dt.int32
+U16 = mybir.dt.uint16
+U8 = mybir.dt.uint8
+FP8X4 = mybir.dt.float8_e4m3fn_x4
+FP4X4 = mybir.dt.float4_e2m1fn_x4
+ACT = mybir.ActivationFunctionType
+ALU = mybir.AluOpType
+
+P = 128
+PASSES = 2
+K_PASS = 512
+PIECE = 256
+GROUP = 128
+
+LOADS = [
+    [(1024, 256), (1024, 352)],
+    [(1024, 1024), (512, 0), (512, 176)],
+    [(1024, 1024), (1024, 512)],
+    [(1024, 1024), (512, 0), (256, 0), (256, 160)],
+]
+
+
+def tile_picked_lsep_none_e_kernel(tc, xT, w1_words, w1_scales, offs, out):
+    nc = tc.nc
+    with ExitStack() as ctx:
+        keep = ctx.enter_context(tc.tile_pool(name="keep", bufs=1))
+        psum = ctx.enter_context(tc.psum_pool(name="psum", bufs=1))
+
+        offsets = keep.tile([P, S // 16], U16, name="offsets")
+        w_words = keep.tile([P, PASSES, 2 * N], U8, name="w_words", align_bytes=64)
+        w_scales = keep.tile([P, PASSES, N], U8, name="w_scales", align_bytes=64)
+
+        nc.gpsimd.memset(w_scales[:].rearrange("p z n -> p (z n)").bitcast(I32), 0)
+
+        rows = xT.rearrange("(z p u e) t -> z u p e t", z=PASSES, p=P, u=2, e=2)
+        raws = {}
+        for i in range(4):
+            t0 = 0
+            for j, (width, unused) in enumerate(LOADS[i]):
+                raw = keep.tile([P, 2, width], F32, name=f"raw{i}_{j}")
+                nc.sync.dma_start(raw[:], rows[i // 2, i % 2, :, :, t0 : t0 + width])
+                raws[i, j] = raw
+                t0 = t0 + width
+                if i == 0 and j == 1:
+                    nc.sync.dma_start(offsets[:], offs)
+                    nc.sync.dma_start(w_words[:].bitcast(I32), w1_words.rearrange("z p b -> p z b").bitcast(I32))
+                    for q in range(4):
+                        nc.sync.dma_start(
+                            w_scales[32 * q : 32 * q + 4].bitcast(I32),
+                            w1_scales[:, 4 * q : 4 * q + 4, :].rearrange("z r n -> r z n").bitcast(I32),
+                        )
+
+        def round_pair(i):
+            pair = keep.tile([P, 2 * T], BF16, name=f"pair{i}")
+            t0 = 0
+            for j, (width, on_scalar) in enumerate(LOADS[i]):
+                src = raws[i, j][:].rearrange("p e t -> p t e")
+                dst = pair[:, 2 * t0 : 2 * (t0 + width)].rearrange("p (t e) -> p t e", e=2)
+                if on_scalar > 0:
+                    nc.scalar.activation(dst[:, :on_scalar, :], src[:, :on_scalar, :], ACT.Copy)
+                if on_scalar < width:
+                    nc.vector.tensor_copy(dst[:, on_scalar:, :], src[:, on_scalar:, :])
+                t0 = t0 + width
+            return pair
+
+        def gather(dst, pair, first, count):
+            nc.vector.tensor_copy(
+                dst, pair[:].bitcast(U32).indirect(offsets[:, first // 16 : (first + count) // 16])
+            )
+
+        def words(woven):
+            return woven[:].bitcast(U32).rearrange("p (n u) -> p n u", u=2)
+
+        pieces = S // PIECE
+        picked0 = [keep.tile([P, 2, PIECE], U32, name=f"picked0_{c}") for c in range(pieces)]
+        woven0 = [keep.tile([P, 4 * PIECE], BF16, name=f"woven0_{c}", align_bytes=64) for c in range(pieces)]
+        codes0 = [keep.tile([P, PIECE], U32, name=f"codes0_{c}", align_bytes=64) for c in range(pieces)]
+        scales0 = [keep.tile([P, PIECE], U8, name=f"scales0_{c}", align_bytes=64) for c in range(pieces)]
+        for u in range(2):
+            pair = round_pair(u)
+            for c in range(pieces):
+                gather(picked0[c][:, u, :], pair, c * PIECE, PIECE)
+        for c in range(pieces):
+            if c < 2:
+                nc.scalar.copy(words(woven0[c]), picked0[c][:].rearrange("p u n -> p n u"))
+            else:
+                nc.vector.tensor_copy(words(woven0[c]), picked0[c][:].rearrange("p u n -> p n u"))
+        for c in range(pieces):
+            nc.vector.quantize_mx(out=codes0[c][:].bitcast(FP8X4), scales=scales0[c][:], in_=woven0[c][:])
+
+        halves = V // PIECE
+        groups = V // GROUP
+        banks_a = [psum.tile([P, 512], F32, name=f"bank_a{h}") for h in range(halves)]
+        banks_b = [psum.tile([P, 512], F32, name=f"bank_b{g}") for g in range(groups)]
+        sums = [banks_a[g // 2][:, (g % 2) * GROUP : (g % 2 + 1) * GROUP] for g in range(groups)]
+        sums = sums + [banks_b[g][:, :GROUP] for g in range(groups)]
+
+        def multiply(g, z, codes, scales):
+            nc.tensor.matmul_mx(
+                out=sums[g],
+                lhsT=w_words[:, z, :].bitcast(FP4X4),
+                lhsT_scale=w_scales[:, z, :],
+                rhs=codes.bitcast(FP8X4),
+                rhs_scale=scales,
+                start=(z == 0),
+                stop=(z == PASSES - 1),
+            )
+
+        def first_pass(g):
+            cols = slice((g % 2) * GROUP, (g % 2 + 1) * GROUP)
+            multiply(g, 0, codes0[g // 2][:, cols], scales0[g // 2][:, cols])
+
+        late = (1, 3)
+        for g in range(2 * groups):
+            if g not in late:
+                first_pass(g)
+
+        picked = [keep.tile([P, 2, PIECE], U32, name=f"picked1_{c}") for c in range(pieces)]
+        pair = round_pair(2)
+        for c in range(pieces):
+            gather(picked[c][:, 0, :], pair, c * PIECE, PIECE)
+        pair = round_pair(3)
+        woven = [keep.tile([P, 4 * PIECE], BF16, name=f"woven1_{c}", align_bytes=64) for c in range(pieces)]
+        for c in range(pieces):
+            gather(picked[c][:, 1, :], pair, c * PIECE, PIECE)
+            nc.scalar.copy(
+                woven[c][:].bitcast(U32).rearrange("p (n u) -> p n u", u=2),
+                picked[c][:].rearrange("p u n -> p n u"),
+            )
+        for c in range(pieces):
+            codes = keep.tile([P, PIECE], U32, name=f"codes1_{c}", align_bytes=64)
+            scales = keep.tile([P, PIECE], U8, name=f"scales1_{c}", align_bytes=64)
+            nc.vector.quantize_mx(out=codes[:].bitcast(FP8X4), scales=scales[:], in_=woven[c][:])
+            multiply(2 * c, 1, codes[:, :GROUP], scales[:, :GROUP])
+            if 2 * c + 1 in late:
+                first_pass(2 * c + 1)
+            multiply(2 * c + 1, 1, codes[:, GROUP:], scales[:, GROUP:])
+
+        first = [keep.tile([P, PIECE], F32, name=f"first{h}") for h in range(halves)]
+        diff = [keep.tile([P, GROUP], F32, name=f"diff{g}") for g in range(groups)]
+        bent = [keep.tile([P, PIECE], F32, name=f"bent{h}") for h in range(halves)]
+        size = [keep.tile([P, PIECE], F32, name=f"size{h}") for h in range(halves)]
+        large = [keep.tile([P, PIECE], F32, name=f"large{h}") for h in range(halves)]
+        soft = [keep.tile([P, PIECE], F32, name=f"soft{h}") for h in range(halves)]
+        result = [keep.tile([P, PIECE], F32, name=f"result{h}") for h in range(halves)]
+        for h in range(halves):
+            nc.scalar.activation(first[h][:], banks_a[h][:, :PIECE], ACT.Copy)
+        for g in range(groups):
+            cols = slice((g % 2) * GROUP, (g % 2 + 1) * GROUP)
+            nc.vector.tensor_tensor(diff[g][:], first[g // 2][:, cols], sums[groups + g], ALU.subtract)
+            nc.scalar.activation(bent[g // 2][:, cols], diff[g][:], ACT.Tanh, scale=0.5)
+        for g in range(groups):
+            cols = slice((g % 2) * GROUP, (g % 2 + 1) * GROUP)
+            nc.vector.tensor_tensor(large[g // 2][:, cols], first[g // 2][:, cols], sums[groups + g], ALU.max)
+        for h in range(halves):
+            nc.vector.scalar_tensor_tensor(size[h][:], bent[h][:], -1.0, bent[h][:], ALU.mult, ALU.max)
+        for h in range(halves):
+            nc.scalar.activation(soft[h][:], size[h][:], ACT.Ln, bias=0.5, scale=0.5)
+            nc.vector.tensor_tensor(result[h][:], large[h][:], soft[h][:], ALU.subtract)
+            nc.sync.dma_start(out[:, h * PIECE : (h + 1) * PIECE], result[h][:])

@@ -23,10 +23,10 @@ PIECE = 256
 GROUP = 128
 
 LOADS = [
-    [(1024, 256), (1024, 352)],
+    [(2048, 672)],
     [(1024, 1024), (512, 0), (512, 176)],
     [(1024, 1024), (1024, 512)],
-    [(1024, 1024), (512, 0), (256, 0), (256, 160)],
+    [(1024, 1024), (512, 0), (512, 256)],
 ]
 
 
@@ -41,6 +41,11 @@ def tile_picked_lsep_none_e_kernel(tc, xT, w1_words, w1_scales, offs, out):
         w_scales = keep.tile([P, PASSES, N], U8, name="w_scales", align_bytes=64)
 
         nc.gpsimd.memset(w_scales[:].rearrange("p z n -> p (z n)").bitcast(I32), 0)
+        for q in range(4):
+            nc.gpsimd.dma_start(
+                w_scales[32 * q : 32 * q + 4].bitcast(I32),
+                w1_scales[:, 4 * q : 4 * q + 4, :].rearrange("z r n -> r z n").bitcast(I32),
+            )
 
         rows = xT.rearrange("(z p u e) t -> z u p e t", z=PASSES, p=P, u=2, e=2)
         raws = {}
@@ -51,14 +56,9 @@ def tile_picked_lsep_none_e_kernel(tc, xT, w1_words, w1_scales, offs, out):
                 nc.sync.dma_start(raw[:], rows[i // 2, i % 2, :, :, t0 : t0 + width])
                 raws[i, j] = raw
                 t0 = t0 + width
-                if i == 0 and j == 1:
+                if i == 0:
                     nc.sync.dma_start(offsets[:], offs)
                     nc.sync.dma_start(w_words[:].bitcast(I32), w1_words.rearrange("z p b -> p z b").bitcast(I32))
-                    for q in range(4):
-                        nc.sync.dma_start(
-                            w_scales[32 * q : 32 * q + 4].bitcast(I32),
-                            w1_scales[:, 4 * q : 4 * q + 4, :].rearrange("z r n -> r z n").bitcast(I32),
-                        )
 
         def round_pair(i):
             pair = keep.tile([P, 2 * T], BF16, name=f"pair{i}")
@@ -146,25 +146,25 @@ def tile_picked_lsep_none_e_kernel(tc, xT, w1_words, w1_scales, offs, out):
                 first_pass(2 * c + 1)
             multiply(2 * c + 1, 1, codes[:, GROUP:], scales[:, GROUP:])
 
-        first = [keep.tile([P, PIECE], F32, name=f"first{h}") for h in range(halves)]
-        diff = [keep.tile([P, GROUP], F32, name=f"diff{g}") for g in range(groups)]
-        bent = [keep.tile([P, PIECE], F32, name=f"bent{h}") for h in range(halves)]
-        size = [keep.tile([P, PIECE], F32, name=f"size{h}") for h in range(halves)]
-        large = [keep.tile([P, PIECE], F32, name=f"large{h}") for h in range(halves)]
-        soft = [keep.tile([P, PIECE], F32, name=f"soft{h}") for h in range(halves)]
-        result = [keep.tile([P, PIECE], F32, name=f"result{h}") for h in range(halves)]
+        first = keep.tile([P, V], F32, name="first")
+        diff = keep.tile([P, V], F32, name="diff")
+        bent = keep.tile([P, V], F32, name="bent")
+        size = keep.tile([P, V], F32, name="size")
+        minus_large = keep.tile([P, V], F32, name="minus_large")
+        soft = keep.tile([P, V], F32, name="soft")
+        result = keep.tile([P, V], F32, name="result")
+        half = [slice(h * PIECE, (h + 1) * PIECE) for h in range(halves)]
         for h in range(halves):
-            nc.scalar.activation(first[h][:], banks_a[h][:, :PIECE], ACT.Copy)
+            nc.scalar.activation(first[:, half[h]], banks_a[h][:, :PIECE], ACT.Copy)
         for g in range(groups):
-            cols = slice((g % 2) * GROUP, (g % 2 + 1) * GROUP)
-            nc.vector.tensor_tensor(diff[g][:], first[g // 2][:, cols], sums[groups + g], ALU.subtract)
-            nc.scalar.activation(bent[g // 2][:, cols], diff[g][:], ACT.Tanh, scale=0.5)
-        for g in range(groups):
-            cols = slice((g % 2) * GROUP, (g % 2 + 1) * GROUP)
-            nc.vector.tensor_tensor(large[g // 2][:, cols], first[g // 2][:, cols], sums[groups + g], ALU.max)
+            cols = slice(g * GROUP, (g + 1) * GROUP)
+            nc.vector.tensor_tensor(diff[:, cols], first[:, cols], sums[groups + g], ALU.subtract)
+            nc.scalar.activation(bent[:, cols], diff[:, cols], ACT.Tanh, scale=0.5)
+        nc.vector.scalar_tensor_tensor(minus_large[:], diff[:], 0.0, first[:], ALU.min, ALU.subtract)
+        nc.vector.scalar_tensor_tensor(size[:], bent[:], -1.0, bent[:], ALU.mult, ALU.max)
         for h in range(halves):
-            nc.vector.scalar_tensor_tensor(size[h][:], bent[h][:], -1.0, bent[h][:], ALU.mult, ALU.max)
-        for h in range(halves):
-            nc.scalar.activation(soft[h][:], size[h][:], ACT.Ln, bias=0.5, scale=0.5)
-            nc.vector.tensor_tensor(result[h][:], large[h][:], soft[h][:], ALU.subtract)
-            nc.sync.dma_start(out[:, h * PIECE : (h + 1) * PIECE], result[h][:])
+            nc.scalar.activation(soft[:, half[h]], size[:, half[h]], ACT.Ln, bias=0.5, scale=0.5)
+            nc.vector.scalar_tensor_tensor(
+                result[:, half[h]], minus_large[:, half[h]], -1.0, soft[:, half[h]], ALU.mult, ALU.subtract
+            )
+            nc.sync.dma_start(out[:, half[h]], result[:, half[h]])

@@ -23,11 +23,13 @@ PIECE = 256
 GROUP = 128
 
 LOADS = [
-    [(2048, 672)],
-    [(1024, 1024), (512, 0), (512, 176)],
-    [(1024, 1024), (1024, 512)],
-    [(1024, 1024), (512, 0), (512, 256)],
+    [(1024, 256), (1024, 352)],
+    [(1024, 1024), (768, 0), (256, 128)],
+    [(1024, 1024), (1024, 320)],
+    [(1024, 1024), (512, 0), (256, 96), (256, 256)],
 ]
+WEAVES = [(0, 256), (256, 256), (512, 256), (768, 128), (896, 128)]
+QUANTS = [(0, 512), (512, 256), (768, 128), (896, 128)]
 
 
 def tile_picked_lsep_none_e_kernel(tc, xT, w1_words, w1_scales, offs, out):
@@ -41,8 +43,9 @@ def tile_picked_lsep_none_e_kernel(tc, xT, w1_words, w1_scales, offs, out):
         w_scales = keep.tile([P, PASSES, N], U8, name="w_scales", align_bytes=64)
 
         nc.gpsimd.memset(w_scales[:].rearrange("p z n -> p (z n)").bitcast(I32), 0)
+        nc.scalar.dma_start(w_words[:].bitcast(I32), w1_words.rearrange("z p b -> p z b").bitcast(I32))
         for q in range(4):
-            nc.gpsimd.dma_start(
+            nc.scalar.dma_start(
                 w_scales[32 * q : 32 * q + 4].bitcast(I32),
                 w1_scales[:, 4 * q : 4 * q + 4, :].rearrange("z r n -> r z n").bitcast(I32),
             )
@@ -52,16 +55,15 @@ def tile_picked_lsep_none_e_kernel(tc, xT, w1_words, w1_scales, offs, out):
         for i in range(4):
             t0 = 0
             for j, (width, unused) in enumerate(LOADS[i]):
-                raw = keep.tile([P, 2, width], F32, name=f"raw{i}_{j}")
+                raw = keep.tile([P, 2, width], F32, name=f"raw{i}_{j}", tag=f"raw{i}_{j}", align_bytes=64)
                 nc.sync.dma_start(raw[:], rows[i // 2, i % 2, :, :, t0 : t0 + width])
                 raws[i, j] = raw
                 t0 = t0 + width
-                if i == 0:
+                if i == 0 and j == 1:
                     nc.sync.dma_start(offsets[:], offs)
-                    nc.sync.dma_start(w_words[:].bitcast(I32), w1_words.rearrange("z p b -> p z b").bitcast(I32))
 
         def round_pair(i):
-            pair = keep.tile([P, 2 * T], BF16, name=f"pair{i}")
+            pair = keep.tile([P, 2 * T], BF16, name=f"pair{i}", tag=f"pair{i}", align_bytes=64)
             t0 = 0
             for j, (width, on_scalar) in enumerate(LOADS[i]):
                 src = raws[i, j][:].rearrange("p e t -> p t e")
@@ -82,32 +84,35 @@ def tile_picked_lsep_none_e_kernel(tc, xT, w1_words, w1_scales, offs, out):
             return woven[:].bitcast(U32).rearrange("p (n u) -> p n u", u=2)
 
         pieces = S // PIECE
-        picked0 = [keep.tile([P, 2, PIECE], U32, name=f"picked0_{c}") for c in range(pieces)]
-        woven0 = [keep.tile([P, 4 * PIECE], BF16, name=f"woven0_{c}", align_bytes=64) for c in range(pieces)]
-        codes0 = [keep.tile([P, PIECE], U32, name=f"codes0_{c}", align_bytes=64) for c in range(pieces)]
-        scales0 = [keep.tile([P, PIECE], U8, name=f"scales0_{c}", align_bytes=64) for c in range(pieces)]
-        for u in range(2):
-            pair = round_pair(u)
-            for c in range(pieces):
-                gather(picked0[c][:, u, :], pair, c * PIECE, PIECE)
+        piece = [slice(c * PIECE, (c + 1) * PIECE) for c in range(pieces)]
+        picked0 = keep.tile([P, 2, S], U32, name="picked0")
+        codes0 = keep.tile([P, S], U32, name="codes0", align_bytes=64)
+        scales0 = keep.tile([P, S], U8, name="scales0", align_bytes=64)
+        gather(picked0[:, 0, :], round_pair(0), 0, S)
+        pair = round_pair(1)
         for c in range(pieces):
-            if c < 2:
-                nc.scalar.copy(words(woven0[c]), picked0[c][:].rearrange("p u n -> p n u"))
-            else:
-                nc.vector.tensor_copy(words(woven0[c]), picked0[c][:].rearrange("p u n -> p n u"))
-        for c in range(pieces):
-            nc.vector.quantize_mx(out=codes0[c][:].bitcast(FP8X4), scales=scales0[c][:], in_=woven0[c][:])
+            gather(picked0[:, 1, piece[c]], pair, c * PIECE, PIECE)
+
+        def quantize0(at, n, woven):
+            nc.vector.quantize_mx(
+                out=codes0[:, at : at + n].bitcast(FP8X4), scales=scales0[:, at : at + n], in_=woven[:]
+            )
+
+        woven_a = keep.tile([P, 4 * V], BF16, name="woven_a", align_bytes=64)
+        woven_b = keep.tile([P, 4 * PIECE], BF16, name="woven_b", align_bytes=64)
+        for c in range(2):
+            nc.scalar.copy(words(woven_a)[:, piece[c], :], picked0[:, :, piece[c]].rearrange("p u n -> p n u"))
+        nc.vector.tensor_copy(words(woven_b), picked0[:, :, piece[2]].rearrange("p u n -> p n u"))
+        quantize0(0, V, woven_a)
+        quantize0(V, PIECE, woven_b)
 
         halves = V // PIECE
         groups = V // GROUP
-        banks_a = [psum.tile([P, 512], F32, name=f"bank_a{h}") for h in range(halves)]
-        banks_b = [psum.tile([P, 512], F32, name=f"bank_b{g}") for g in range(groups)]
-        sums = [banks_a[g // 2][:, (g % 2) * GROUP : (g % 2 + 1) * GROUP] for g in range(groups)]
-        sums = sums + [banks_b[g][:, :GROUP] for g in range(groups)]
+        sums = [psum.tile([P, GROUP], F32, name=f"sums{g}") for g in range(2 * groups)]
 
         def multiply(g, z, codes, scales):
             nc.tensor.matmul_mx(
-                out=sums[g],
+                out=sums[g][:],
                 lhsT=w_words[:, z, :].bitcast(FP4X4),
                 lhsT_scale=w_scales[:, z, :],
                 rhs=codes.bitcast(FP8X4),
@@ -117,34 +122,36 @@ def tile_picked_lsep_none_e_kernel(tc, xT, w1_words, w1_scales, offs, out):
             )
 
         def first_pass(g):
-            cols = slice((g % 2) * GROUP, (g % 2 + 1) * GROUP)
-            multiply(g, 0, codes0[g // 2][:, cols], scales0[g // 2][:, cols])
+            cols = slice(g * GROUP, (g + 1) * GROUP)
+            multiply(g, 0, codes0[:, cols], scales0[:, cols])
 
-        late = (1, 3)
-        for g in range(2 * groups):
-            if g not in late:
-                first_pass(g)
+        for g in range(2 * groups - 2):
+            first_pass(g)
 
-        picked = [keep.tile([P, 2, PIECE], U32, name=f"picked1_{c}") for c in range(pieces)]
-        pair = round_pair(2)
-        for c in range(pieces):
-            gather(picked[c][:, 0, :], pair, c * PIECE, PIECE)
+        picked1 = keep.tile([P, 2, S], U32, name="picked1")
+        gather(picked1[:, 0, :], round_pair(2), 0, S)
+        woven_c = keep.tile([P, 4 * PIECE], BF16, name="woven_c", tag="raw2_1", align_bytes=64)
+        nc.scalar.copy(words(woven_c), picked0[:, :, piece[3]].rearrange("p u n -> p n u"))
+        quantize0(V + PIECE, PIECE, woven_c)
+        for g in range(2 * groups - 2, 2 * groups):
+            first_pass(g)
         pair = round_pair(3)
-        woven = [keep.tile([P, 4 * PIECE], BF16, name=f"woven1_{c}", align_bytes=64) for c in range(pieces)]
+        woven1 = keep.tile([P, 4 * S], BF16, name="woven1", align_bytes=64)
+        codes1 = keep.tile([P, S], U32, name="codes1", align_bytes=64)
+        scales1 = keep.tile([P, S], U8, name="scales1", align_bytes=64)
         for c in range(pieces):
-            gather(picked[c][:, 1, :], pair, c * PIECE, PIECE)
-            nc.scalar.copy(
-                woven[c][:].bitcast(U32).rearrange("p (n u) -> p n u", u=2),
-                picked[c][:].rearrange("p u n -> p n u"),
+            gather(picked1[:, 1, piece[c]], pair, c * PIECE, PIECE)
+        for at, n in WEAVES:
+            nc.scalar.copy(words(woven1)[:, at : at + n, :], picked1[:, :, at : at + n].rearrange("p u n -> p n u"))
+        for at, n in QUANTS:
+            nc.vector.quantize_mx(
+                out=codes1[:, at : at + n].bitcast(FP8X4),
+                scales=scales1[:, at : at + n],
+                in_=woven1[:, 4 * at : 4 * (at + n)],
             )
-        for c in range(pieces):
-            codes = keep.tile([P, PIECE], U32, name=f"codes1_{c}", align_bytes=64)
-            scales = keep.tile([P, PIECE], U8, name=f"scales1_{c}", align_bytes=64)
-            nc.vector.quantize_mx(out=codes[:].bitcast(FP8X4), scales=scales[:], in_=woven[c][:])
-            multiply(2 * c, 1, codes[:, :GROUP], scales[:, :GROUP])
-            if 2 * c + 1 in late:
-                first_pass(2 * c + 1)
-            multiply(2 * c + 1, 1, codes[:, GROUP:], scales[:, GROUP:])
+            for g in range(at // GROUP, (at + n) // GROUP):
+                cols = slice(g * GROUP, (g + 1) * GROUP)
+                multiply(g, 1, codes1[:, cols], scales1[:, cols])
 
         first = keep.tile([P, V], F32, name="first")
         diff = keep.tile([P, V], F32, name="diff")
@@ -154,11 +161,11 @@ def tile_picked_lsep_none_e_kernel(tc, xT, w1_words, w1_scales, offs, out):
         soft = keep.tile([P, V], F32, name="soft")
         result = keep.tile([P, V], F32, name="result")
         half = [slice(h * PIECE, (h + 1) * PIECE) for h in range(halves)]
-        for h in range(halves):
-            nc.scalar.activation(first[:, half[h]], banks_a[h][:, :PIECE], ACT.Copy)
+        for g in range(groups):
+            nc.scalar.activation(first[:, g * GROUP : (g + 1) * GROUP], sums[g][:], ACT.Copy)
         for g in range(groups):
             cols = slice(g * GROUP, (g + 1) * GROUP)
-            nc.vector.tensor_tensor(diff[:, cols], first[:, cols], sums[groups + g], ALU.subtract)
+            nc.vector.tensor_tensor(diff[:, cols], first[:, cols], sums[groups + g][:], ALU.subtract)
             nc.scalar.activation(bent[:, cols], diff[:, cols], ACT.Tanh, scale=0.5)
         nc.vector.scalar_tensor_tensor(minus_large[:], diff[:], 0.0, first[:], ALU.min, ALU.subtract)
         nc.vector.scalar_tensor_tensor(size[:], bent[:], -1.0, bent[:], ALU.mult, ALU.max)

from contextlib import ExitStack

import concourse.mybir as mybir

K, T, S, V, N = 1024, 2048, 1024, 512, 128
FLOPS = 2 * K * S * N

F32 = mybir.dt.float32
BF16 = mybir.dt.bfloat16
U32 = mybir.dt.uint32
I32 = mybir.dt.int32
U16 = mybir.dt.uint16
U8 = mybir.dt.uint8
FP8X4 = mybir.dt.float8_e4m3fn_x4
FP4X4 = mybir.dt.float4_e2m1fn_x4
ACT = mybir.ActivationFunctionType
ALU = mybir.AluOpType

P = 128
PASSES = 2
K_PASS = 512
PIECE = 256
GROUP = 128

LOADS = [
    [(1024, 256), (1024, 352)],
    [(1024, 1024), (768, 0), (256, 128)],
    [(1024, 1024), (1024, 320)],
    [(1024, 1024), (512, 0), (256, 96), (256, 256)],
]
WEAVES = [(0, 256), (256, 256), (512, 256), (768, 128), (896, 128)]
QUANTS = [(0, 512), (512, 256), (768, 128), (896, 128)]


def tile_picked_lsep_none_e_kernel(tc, xT, w1_words, w1_scales, offs, out):
    nc = tc.nc
    with ExitStack() as ctx:
        keep = ctx.enter_context(tc.tile_pool(name="keep", bufs=1))
        psum = ctx.enter_context(tc.psum_pool(name="psum", bufs=1))

        offsets = keep.tile([P, S // 16], U16, name="offsets")
        w_words = keep.tile([P, PASSES, 2 * N], U8, name="w_words", align_bytes=64)
        w_scales = keep.tile([P, PASSES, N], U8, name="w_scales", align_bytes=64)

        nc.gpsimd.memset(w_scales[:].rearrange("p z n -> p (z n)").bitcast(I32), 0)
        nc.scalar.dma_start(w_words[:].bitcast(I32), w1_words.rearrange("z p b -> p z b").bitcast(I32))
        for q in range(4):
            nc.scalar.dma_start(
                w_scales[32 * q : 32 * q + 4].bitcast(I32),
                w1_scales[:, 4 * q : 4 * q + 4, :].rearrange("z r n -> r z n").bitcast(I32),
            )

        rows = xT.rearrange("(z p u e) t -> z u p e t", z=PASSES, p=P, u=2, e=2)
        raws = {}
        for i in range(4):
            t0 = 0
            for j, (width, unused) in enumerate(LOADS[i]):
                raw = keep.tile([P, 2, width], F32, name=f"raw{i}_{j}", tag=f"raw{i}_{j}", align_bytes=64)
                nc.sync.dma_start(raw[:], rows[i // 2, i % 2, :, :, t0 : t0 + width])
                raws[i, j] = raw
                t0 = t0 + width
                if i == 0 and j == 1:
                    nc.sync.dma_start(offsets[:], offs)

        def round_pair(i):
            pair = keep.tile([P, 2 * T], BF16, name=f"pair{i}", tag=f"pair{i}", align_bytes=64)
            t0 = 0
            for j, (width, on_scalar) in enumerate(LOADS[i]):
                src = raws[i, j][:].rearrange("p e t -> p t e")
                dst = pair[:, 2 * t0 : 2 * (t0 + width)].rearrange("p (t e) -> p t e", e=2)
                if on_scalar > 0:
                    nc.scalar.activation(dst[:, :on_scalar, :], src[:, :on_scalar, :], ACT.Copy)
                if on_scalar < width:
                    nc.vector.tensor_copy(dst[:, on_scalar:, :], src[:, on_scalar:, :])
                t0 = t0 + width
            return pair

        def gather(dst, pair, first, count):
            nc.vector.tensor_copy(
                dst, pair[:].bitcast(U32).indirect(offsets[:, first // 16 : (first + count) // 16])
            )

        def words(woven):
            return woven[:].bitcast(U32).rearrange("p (n u) -> p n u", u=2)

        pieces = S // PIECE
        piece = [slice(c * PIECE, (c + 1) * PIECE) for c in range(pieces)]
        picked0 = keep.tile([P, 2, S], U32, name="picked0")
        codes0 = keep.tile([P, S], U32, name="codes0", align_bytes=64)
        scales0 = keep.tile([P, S], U8, name="scales0", align_bytes=64)
        gather(picked0[:, 0, :], round_pair(0), 0, S)
        pair = round_pair(1)
        for c in range(pieces):
            gather(picked0[:, 1, piece[c]], pair, c * PIECE, PIECE)

        def quantize0(at, n, woven):
            nc.vector.quantize_mx(
                out=codes0[:, at : at + n].bitcast(FP8X4), scales=scales0[:, at : at + n], in_=woven[:]
            )

        woven_a = keep.tile([P, 4 * V], BF16, name="woven_a", align_bytes=64)
        woven_b = keep.tile([P, 4 * PIECE], BF16, name="woven_b", align_bytes=64)
        for c in range(2):
            nc.scalar.copy(words(woven_a)[:, piece[c], :], picked0[:, :, piece[c]].rearrange("p u n -> p n u"))
        nc.vector.tensor_copy(words(woven_b), picked0[:, :, piece[2]].rearrange("p u n -> p n u"))
        quantize0(0, V, woven_a)
        quantize0(V, PIECE, woven_b)

        halves = V // PIECE
        groups = V // GROUP
        sums = [psum.tile([P, GROUP], F32, name=f"sums{g}") for g in range(2 * groups)]

        def multiply(g, z, codes, scales):
            nc.tensor.matmul_mx(
                out=sums[g][:],
                lhsT=w_words[:, z, :].bitcast(FP4X4),
                lhsT_scale=w_scales[:, z, :],
                rhs=codes.bitcast(FP8X4),
                rhs_scale=scales,
                start=(z == 0),
                stop=(z == PASSES - 1),
            )

        def first_pass(g):
            cols = slice(g * GROUP, (g + 1) * GROUP)
            multiply(g, 0, codes0[:, cols], scales0[:, cols])

        for g in range(2 * groups - 2):
            first_pass(g)

        picked1 = keep.tile([P, 2, S], U32, name="picked1")
        gather(picked1[:, 0, :], round_pair(2), 0, S)
        woven_c = keep.tile([P, 4 * PIECE], BF16, name="woven_c", tag="raw2_1", align_bytes=64)
        nc.scalar.copy(words(woven_c), picked0[:, :, piece[3]].rearrange("p u n -> p n u"))
        quantize0(V + PIECE, PIECE, woven_c)
        for g in range(2 * groups - 2, 2 * groups):
            first_pass(g)
        pair = round_pair(3)
        woven1 = keep.tile([P, 4 * S], BF16, name="woven1", align_bytes=64)
        codes1 = keep.tile([P, S], U32, name="codes1", align_bytes=64)
        scales1 = keep.tile([P, S], U8, name="scales1", align_bytes=64)
        for c in range(pieces):
            gather(picked1[:, 1, piece[c]], pair, c * PIECE, PIECE)
        for at, n in WEAVES:
            nc.scalar.copy(words(woven1)[:, at : at + n, :], picked1[:, :, at : at + n].rearrange("p u n -> p n u"))
        for at, n in QUANTS:
            nc.vector.quantize_mx(
                out=codes1[:, at : at + n].bitcast(FP8X4),
                scales=scales1[:, at : at + n],
                in_=woven1[:, 4 * at : 4 * (at + n)],
            )
            for g in range(at // GROUP, (at + n) // GROUP):
                cols = slice(g * GROUP, (g + 1) * GROUP)
                multiply(g, 1, codes1[:, cols], scales1[:, cols])

        first = keep.tile([P, V], F32, name="first")
        diff = keep.tile([P, V], F32, name="diff")
        bent = keep.tile([P, V], F32, name="bent")
        size = keep.tile([P, V], F32, name="size")
        minus_large = keep.tile([P, V], F32, name="minus_large")
        soft = keep.tile([P, V], F32, name="soft")
        result = keep.tile([P, V], F32, name="result")
        half = [slice(h * PIECE, (h + 1) * PIECE) for h in range(halves)]
        for g in range(groups):
            nc.scalar.activation(first[:, g * GROUP : (g + 1) * GROUP], sums[g][:], ACT.Copy)
        for g in range(groups):
            cols = slice(g * GROUP, (g + 1) * GROUP)
            nc.vector.tensor_tensor(diff[:, cols], first[:, cols], sums[groups + g][:], ALU.subtract)
            nc.scalar.activation(bent[:, cols], diff[:, cols], ACT.Tanh, scale=0.5)
        nc.vector.scalar_tensor_tensor(minus_large[:], diff[:], 0.0, first[:], ALU.min, ALU.subtract)
        nc.vector.scalar_tensor_tensor(size[:], bent[:], -1.0, bent[:], ALU.mult, ALU.max)
        for h in range(halves):
            nc.scalar.activation(soft[:, half[h]], size[:, half[h]], ACT.Ln, bias=0.5, scale=0.5)
            nc.vector.scalar_tensor_tensor(
                result[:, half[h]], minus_large[:, half[h]], -1.0, soft[:, half[h]], ALU.mult, ALU.subtract
            )
            nc.sync.dma_start(out[:, half[h]], result[:, half[h]])
